import numpy as np
import ml_dtypes


def mxq(x, axis, fmt="e4m3"):
    dtype, down = {"e4m3": (ml_dtypes.float8_e4m3fn, 7), "e5m2": (ml_dtypes.float8_e5m2, 14)}[fmt]
    v = np.moveaxis(np.asarray(x, np.float32).astype(ml_dtypes.bfloat16).astype(np.float64), axis, -1)
    blocks = v.reshape(v.shape[:-1] + (-1, 32))
    amax = np.abs(blocks).max(-1, keepdims=True)
    byte = np.maximum(np.where(amax > 0, np.frexp(amax)[1] - 1 + 127, 0) - down, 1)
    scale = np.exp2(byte - 127.0)
    codes = (blocks / scale).astype(np.float32).astype(dtype).astype(np.float64)
    return np.moveaxis((codes * scale).reshape(v.shape), -1, axis)


WIDE = False


def mx_kscale(k):
    if not WIDE:
        return np.ones(k)
    levels = np.array([10, -10, 5, -5, 0])
    if k % 512:
        return np.exp2(np.random.permutation(np.resize(levels, k // 32))).repeat(32)
    a = np.empty((k // 512, 16))
    for p in range(k // 512):
        a[p, :8] = np.random.permutation(np.resize(levels, 8))
        for g in range(8):
            far = levels[np.abs(levels - a[p, g]) >= 10]
            a[p, g + 8] = far[np.random.randint(len(far))]
    return np.exp2(a.ravel()).repeat(32)


BF16 = ml_dtypes.bfloat16


def bf(x):
    return np.asarray(x, np.float32).astype(BF16)


def f64(x):
    return np.asarray(x).astype(np.float64)


E2M1 = np.array([0.0, 0.5, 1.0, 1.5, 2.0, 3.0, 4.0, 6.0, -0.0, -0.5, -1.0, -1.5, -2.0, -3.0, -4.0, -6.0])


def pack_weight(w, fmt):
    k, n = w.shape
    w = f64(bf(w)).reshape(k // 32, 32, n)
    amax = np.abs(w).max(1)
    if fmt == "e4m3":
        byte = np.frexp(amax)[1] - 1 + 127 - 7
    else:
        mant, ex = np.frexp(amax / 6.0)
        byte = np.where(mant > 0.5, ex, ex - 1) + 127
    byte = np.clip(np.where(amax > 0, byte, 1), 1, 254)
    scaled = (w * np.exp2(127.0 - byte)[:, None, :]).reshape(k, n).astype(np.float32)
    by_word = np.ascontiguousarray(scaled.reshape(k // 512, 128, 4, n).transpose(0, 1, 3, 2))
    if fmt == "e4m3":
        words = by_word.astype(ml_dtypes.float8_e4m3fn).view(np.uint8)
    else:
        c = by_word.astype(ml_dtypes.float4_e2m1fn).view(np.uint8) & 0xF
        words = c[..., 0::2] | (c[..., 1::2] << 4)
    return np.ascontiguousarray(words), np.ascontiguousarray(byte.astype(np.uint8).reshape(k // 512, 16, n))


def unpack_weight(words, scales, fmt):
    g, p, n, _ = words.shape
    if fmt == "e4m3":
        vals = np.ascontiguousarray(words).view(ml_dtypes.float8_e4m3fn).astype(np.float64)
    else:
        nib = np.empty((g, p, n, 4), np.uint8)
        nib[..., 0::2] = words & 0xF
        nib[..., 1::2] = words >> 4
        vals = E2M1[nib]
    vals = vals * np.repeat(np.exp2(scales.astype(np.float64) - 127.0), 8, axis=1)[..., None]
    return vals.transpose(0, 1, 3, 2).reshape(g * 512, n)
def pack4(w):
    words, scales = pack_weight(w, "e2m1")
    return words.reshape(words.shape[0], 128, -1), scales


def unpack4(words, scales):
    return unpack_weight(words.reshape(words.shape[0], 128, -1, 2), scales, "e2m1")


E4M3FN = np.array([(-1.0 if i & 128 else 1.0) * ((1.0 + (i & 7) / 8.0) * 2.0 ** (((i >> 3) & 15) - 7) if i & 120 else (i & 7) * 2.0 ** -9) for i in range(256)])


def e4m3fn_bytes(y):
    return np.clip(np.asarray(y, np.float64), -448.0, 448.0).astype(np.float32).astype(ml_dtypes.float8_e4m3fn).view(np.uint8)


def e4m3fn_values(b):
    return E4M3FN[b]


T, S, H, D, C = 1024, 1024, 8, 128, 1536


def setup_inputs():
    s = mx_kscale(T)
    t = mx_kscale(H * D)
    e = np.exp(np.random.standard_normal((H, T, S)))
    probs = e / e.sum(axis=2, keepdims=True)
    do = np.random.standard_normal((T, H * D)) * S / np.sqrt(T) / s[:, None]
    do_scale = (np.abs(do.reshape(T, H, D)).max(axis=2) / 448).astype(np.float32)
    do_bytes = e4m3fn_bytes(do / np.repeat(do_scale.astype(np.float64), D, axis=1))
    w_words, w_scales = pack4(np.random.standard_normal((H * D, C)) / np.sqrt(H * D) / t[:, None])
    return {"attn": bf(probs * s[None, :, None]),
            "do_bytes": do_bytes,
            "do_scale": do_scale,
            "lv": bf((1 + 0.1 * np.random.standard_normal(H * D)) * t),
            "w_words": w_words,
            "w_scales": w_scales}


def reference(attn, do_bytes, do_scale, lv, w_words, w_scales):
    do = e4m3fn_values(do_bytes) * np.repeat(f64(do_scale), D, axis=1)
    aq = mxq(f64(attn), 1, "e4m3").swapaxes(1, 2)
    dq = mxq(do, 0, "e4m3").reshape(T, H, D).transpose(1, 0, 2)
    dv = aq @ dq
    dv = dv.transpose(1, 0, 2).reshape(S, H * D)
    du = dv * f64(lv)
    dx = mxq(du, 1, "e4m3") @ unpack4(w_words, w_scales)
    return dv, dx

from contextlib import ExitStack

import concourse.mybir as mybir
from concourse.masks import make_identity

F32 = mybir.dt.float32
BF16 = mybir.dt.bfloat16
I32 = mybir.dt.int32
U32 = mybir.dt.uint32
U8 = mybir.dt.uint8
FP8 = mybir.dt.float8_e4m3fn
FP8X4 = mybir.dt.float8_e4m3fn_x4
FP4X4 = mybir.dt.float4_e2m1fn_x4
COPY = mybir.ActivationFunctionType.Copy
MULT = mybir.AluOpType.mult

P = 128
T = 1024
S = 1024
H = 8
D = 128
C = 1536
CH = H * D
PACK = 4
G = 2
NB = 512
SECTIONS = ((0, 512), (512, 256), (768, 128), (896, 128))
LEAD = 2
DX_START = (1, 4, 1, 0)
HEAD_ORDER = [(0, 0), (0, 1), (0, 2), (0, 3), (1, 0), (0, 4), (0, 5), (1, 1), (0, 6), (0, 7)] + [(1, h) for h in range(2, 8)] + [(2, h) for h in range(8)] + [(3, h) for h in range(8)]

FLOPS = 2 * T * S * CH + 2 * S * CH * C


def tile_attention_value_gradient_d4_kernel(tc, attn, do_bytes, do_scale, lv, w_words, w_scales, out_0, out_1):
    nc = tc.nc
    load = {"v": 0.0, "s": 0.0}

    def lighter(v_cost, s_cost):
        if load["v"] + v_cost <= load["s"] + s_cost:
            load["v"] += v_cost
            return "v"
        load["s"] += s_cost
        return "s"

    def copy_on(engine, out, in_):
        if engine == "v":
            nc.vector.tensor_copy(out=out, in_=in_)
        else:
            nc.scalar.copy(out=out, in_=in_)

    with ExitStack() as ctx:

        const = ctx.enter_context(tc.tile_pool(name="const", bufs=1))
        raw_pool = ctx.enter_context(tc.tile_pool(name="raw", bufs=H))
        grp_pool = ctx.enter_context(tc.tile_pool(name="grp", bufs=6))
        code_pool = ctx.enter_context(tc.tile_pool(name="code", bufs=4))
        du_pool = ctx.enter_context(tc.tile_pool(name="du", bufs=3))
        dv_pool = ctx.enter_context(tc.tile_pool(name="dv", bufs=2))
        dv_psum = ctx.enter_context(tc.psum_pool(name="dvp", bufs=2))
        tr_psum = ctx.enter_context(tc.psum_pool(name="trp", bufs=2))
        dx_psum = ctx.enter_context(tc.psum_pool(name="dxp", bufs=4))

        scale_sb = const.tile([P, G, PACK, H], F32, name="scale_sb")
        nc.sync.dma_start(out=scale_sb[:].rearrange("p g t h -> p g (t h)"), in_=do_scale.rearrange("(g p t) h -> p g (t h)", g=G, t=PACK))

        do_codes = const.tile([P, G, CH], U32, name="do_codes", align_bytes=64)
        do_scales = const.tile([P, G, CH], U8, name="do_scales", align_bytes=64)
        ident = const.tile([P, P], F32, name="ident")
        lv_bf = const.tile([P, G, PACK], BF16, name="lv_bf")
        lv_sb = const.tile([P, G, PACK], F32, name="lv_sb")
        w_sb = const.tile([P, G, 2 * C], U8, name="w_sb", align_bytes=64)
        ws_sb = const.tile([P, G, C], U8, name="ws_sb", align_bytes=64)

        raw = {}

        def load_attn(h, g):
            if h not in raw:
                raw_tile = raw_pool.tile([P, G, PACK, S], BF16, name="raw")
                raw[h] = raw_tile
            nc.sync.dma_start(out=raw[h][:, g, :, :], in_=attn[h].rearrange("(g p t) s -> g p t s", g=G, t=PACK)[g])

        def quantize(grouped, codes, scales):
            nc.vector.quantize_mx(out=codes.bitcast(FP8X4), scales=scales, in_=grouped)
            load["v"] += grouped.shape[1] * 0.222 + 50

        def interleave(out, in_, engine=None):
            n = in_.shape[1] * in_.shape[2]
            copy_on(
                engine or lighter(0.51 * n + 50, 0.96 * n + 40),
                out.rearrange("p (c i t) -> p c t i", i=4, t=PACK),
                in_.rearrange("p t (c i) -> p c t i", i=4),
            )

        units = []
        for sec, h in HEAD_ORDER:
            if SECTIONS[sec][1] == NB:
                units.append((sec, h, (0,)))
                units.append((sec, h, (1,)))
            else:
                units.append((sec, h, (0, 1)))
        grouped_of = {}

        def interleave_unit(u):
            sec, h, gs = units[u]
            s0, keys = SECTIONS[sec]
            grouped = grp_pool.tile([P, NB * PACK], BF16, name="grouped", align_bytes=64)
            n = keys * PACK * len(gs)
            if len(gs) == 1:
                interleave(grouped[:, :n], raw[h][:, gs[0], :, s0 : s0 + keys])
            else:
                copy_on(
                    lighter(0.51 * n + 50, 0.96 * n + 40),
                    grouped[:, :n].rearrange("p (g s t) -> p g s t", g=G, t=PACK),
                    raw[h][:, :, :, s0 : s0 + keys].rearrange("p g t s -> p g s t"),
                )
            grouped_of[u] = grouped

        with tc.tile_pool(name="dost", bufs=2) as do_pool:
            do_raw = []
            for g in range(G):
                b = do_pool.tile([P, PACK, CH], U8, name="do_b")
                nc.sync.dma_start(out=b[:], in_=do_bytes.rearrange("(g p t) c -> g p t c", g=G, t=PACK)[g])
                do_raw.append(b)
                load_attn(0, g)
            nc.sync.dma_start(out=lv_bf[:], in_=lv.rearrange("(g p t) -> p g t", g=G, t=PACK))
            load_attn(1, 0)
            load_attn(1, 1)
            make_identity(nc, ident[:])
            nc.gpsimd.memset(ws_sb[:].bitcast(I32), 0)
            waiting = []
            for g in range(G):
                if g == 1:
                    for u in range(1):
                        interleave_unit(u)
                for half in range(2):
                    plane = do_pool.tile([P, PACK, NB], BF16, name="do_plane")
                    for t in range(PACK):
                        for hh in range(4):
                            h = half * 4 + hh
                            src = do_raw[g][:, t, h * D : (h + 1) * D].bitcast(FP8)
                            dst = plane[:, t, hh * D : (hh + 1) * D]
                            sc = scale_sb[:, g, t, h : h + 1]
                            if t < 2:
                                nc.scalar.activation(out=dst, in_=src, func=COPY, scale=sc)
                                load["s"] += 107 + 40
                            else:
                                nc.vector.tensor_scalar(out=dst, in0=src, scalar1=sc, scalar2=None, op0=MULT)
                                load["v"] += 54 + 50
                    grouped = grp_pool.tile([P, NB * PACK], BF16, name="grouped", align_bytes=64)
                    interleave(grouped[:], plane[:])
                    if waiting:
                        quantize(*waiting.pop())
                    waiting.append((grouped[:], do_codes[:, g, half * NB : (half + 1) * NB], do_scales[:, g, half * NB : (half + 1) * NB]))

        dx_pool = ctx.enter_context(tc.tile_pool(name="dx", bufs=2))
        for h in range(2, H):
            for g in range(G):
                load_attn(h, g)
            if h == 7:
                nc.sync.dma_start(out=w_sb[:].bitcast(I32), in_=w_words.rearrange("g p b -> p g b").bitcast(I32))
                for q in range(4):
                    nc.sync.dma_start(
                        out=ws_sb[32 * q : 32 * q + 4, :, :].bitcast(I32),
                        in_=w_scales[:, 4 * q : 4 * q + 4, :].rearrange("g q c -> q g c").bitcast(I32),
                    )

        at = {}

        def schedule(step, fn):
            at.setdefault(step, []).append(fn)

        codes_of = {}
        dv_of = {}
        halves_of = {}
        bank_of = {}
        dx_banks = {}

        def quantize_unit(u):
            sec, h, gs = units[u]
            s0, keys = SECTIONS[sec]
            n = keys * len(gs)
            cd = code_pool.tile([P, NB], U32, name="codes", align_bytes=64)
            sc = code_pool.tile([P, NB], U8, name="scales", align_bytes=64)
            quantize(grouped_of.pop(u)[:, : n * PACK], cd[:, :n], sc[:, :n])
            for i, g in enumerate(gs):
                codes_of[sec, h, g] = (cd[:, i * keys : (i + 1) * keys], sc[:, i * keys : (i + 1) * keys])

        def stage_one(sec, h, u):
            s0, keys = SECTIONS[sec]
            n_kt = keys // P
            per = 4 // n_kt
            half = h // 4
            hh = h % 4
            if hh == 0:
                if n_kt == 4:
                    dv_tile = dv_pool.tile([P, 4, NB], F32, name="dv_4")
                elif n_kt == 2:
                    dv_tile = dv_pool.tile([P, 2, NB], F32, name="dv_2")
                else:
                    dv_tile = dv_pool.tile([P, 1, NB], F32, name="dv_1")
                dv_of[sec, half] = dv_tile
            dv = dv_of[sec, half]
            if hh % per == 0:
                dv_bank = dv_psum.tile([P, n_kt, per, D], F32, name="dv_bank")
                bank_of[sec] = dv_bank
            bank = bank_of[sec]
            for kt in range(n_kt):
                for g in range(G):
                    cd, sc = codes_of[sec, h, g]
                    nc.tensor.matmul_mx(
                        out=bank[:, kt, hh % per, :],
                        lhsT=cd[:, kt * P : (kt + 1) * P].bitcast(FP8X4),
                        lhsT_scale=sc[:, kt * P : (kt + 1) * P],
                        rhs=do_codes[:, g, h * D : (h + 1) * D].bitcast(FP8X4),
                        rhs_scale=do_scales[:, g, h * D : (h + 1) * D],
                        start=g == 0,
                        stop=g == G - 1,
                    )
            if hh % per == per - 1:
                first = hh - per + 1

                def empty_dv():
                    copy_on(
                        lighter(427 + 50, 427 + 40),
                        dv[:, :, first * D : (hh + 1) * D],
                        bank[:].rearrange("p k h d -> p k (h d)"),
                    )

                schedule(u + 1, empty_dv)
            if hh == 3:
                after_half(sec, half, dv, u)

        def turn(kt, dv):
            bank = tr_psum.tile([P, PACK, P], F32, name="tr_bank")
            for t in range(PACK):
                nc.tensor.transpose(bank[:, t, :], dv[:, kt, t::PACK], ident[:])
            return bank

        def scale_du(kt, half, du, bank):
            nc.vector.tensor_tensor(
                out=du[:, kt * NB : (kt + 1) * NB].rearrange("p (n t) -> p n t", t=PACK),
                in0=bank[:].rearrange("p t n -> p n t"),
                in1=lv_sb[:, half, :].unsqueeze(1).to_broadcast([P, P, PACK]),
                op=MULT,
            )
            load["v"] += 427 + 50

        def stage_two(kt, halves, which, banks):
            for n in range(C // NB):
                if 0 in which:
                    dx_bank = dx_psum.tile([P, NB], F32, name="dx_bank")
                    banks.append(dx_bank)
                for half in which:
                    cd, sc = halves[half]
                    nc.tensor.matmul_mx(
                        out=banks[n][:],
                        lhsT=cd[:, kt * P : (kt + 1) * P].bitcast(FP8X4),
                        lhsT_scale=sc[:, kt * P : (kt + 1) * P],
                        rhs=w_sb[:, half, 2 * n * NB : 2 * (n + 1) * NB].bitcast(FP4X4),
                        rhs_scale=ws_sb[:, half, n * NB : (n + 1) * NB],
                        start=half == 0,
                        stop=half == 1,
                    )

        def empty_dx(row, banks, last):
            dx = dx_pool.tile([P, C], F32, name="dx")
            for n in range(C // NB):
                copy_on(lighter(427 + 50, 427 + 40), dx[:, n * NB : (n + 1) * NB], banks[n][:])
                if last:
                    nc.sync.dma_start(out=out_1[row : row + P, n * NB : (n + 1) * NB], in_=dx[:, n * NB : (n + 1) * NB])
            if not last:
                nc.sync.dma_start(out=out_1[row : row + P, :], in_=dx[:])

        last_sec = HEAD_ORDER[-1][0]

        def after_half(sec, half, dv, u):
            s0, keys = SECTIONS[sec]
            n_kt = keys // P
            halves = halves_of.setdefault(sec, {})
            state = {}

            def store_dv():
                nc.sync.dma_start(
                    out=out_0[s0 : s0 + keys, half * NB : (half + 1) * NB].rearrange("(k p) c -> p k c", p=P),
                    in_=dv[:],
                )

            def open_du():
                grouped = grp_pool.tile([P, NB * PACK], BF16, name="grouped", align_bytes=64)
                state["du"] = grouped

            def close_du():
                cd = du_pool.tile([P, NB], U32, name="du_codes", align_bytes=64)
                sc = du_pool.tile([P, NB], U8, name="du_scales", align_bytes=64)
                quantize(state["du"][:, : keys * PACK], cd[:, :keys], sc[:, :keys])
                halves[half] = (cd, sc)

            def do_turn(kt):
                state[kt] = turn(kt, dv)

            def do_scale(kt):
                scale_du(kt, half, state["du"], state.pop(kt))

            schedule(u + 1, store_dv)
            lag = 3
            first = u + lag
            schedule(first, open_du)
            for kt in range(n_kt):
                schedule(first + kt, lambda kt=kt: do_turn(kt))
                schedule(first + kt + 1, lambda kt=kt: do_scale(kt))
            done = first + n_kt + 1
            schedule(done, close_du)

            def do_two(kt, which):
                stage_two(kt, halves, which, dx_banks.setdefault((sec, kt), []))

            def do_empty(kt):
                empty_dx(s0 + kt * P, dx_banks.pop((sec, kt)), sec == last_sec)

            early = sec == last_sec and n_kt == 1
            if early:
                schedule(done + DX_START[sec], lambda: do_two(0, (half,)))
                if half == 1:
                    schedule(done + DX_START[sec] + 1, lambda: do_empty(0))
            elif half == 1:
                for kt in range(n_kt):
                    schedule(done + DX_START[sec] + 1 * kt, lambda kt=kt: do_two(kt, (0, 1)))
                    schedule(done + DX_START[sec] + 1 * kt + 1, lambda kt=kt: do_empty(kt))

        for u in range(1, LEAD):
            interleave_unit(u)
        quantize(*waiting.pop())
        nc.vector.tensor_copy(out=lv_sb[:], in_=lv_bf[:])
        u = 0
        while u < len(units) or at:
            if u + LEAD < len(units):
                interleave_unit(u + LEAD)
            for fn in at.pop(u, []):
                fn()
            if u < len(units):
                quantize_unit(u)
                sec, h, gs = units[u]
                if gs[-1] == G - 1:
                    stage_one(sec, h, u)
            u += 1
